import numpy as np, ml_dtypes
CORES = [76,84,92,100,108,116,124]
N = 7
S, B = 4, 256
def setup_inputs(rng):
    a = (rng.standard_normal((128, 128), dtype=np.float32) / 8).astype(ml_dtypes.bfloat16)
    return {"x": (rng.standard_normal((N, 128, S * B), dtype=np.float32) / 2).astype(ml_dtypes.bfloat16), "a": np.broadcast_to(a, (N, 128, 128)).copy()}
def reference(x, a):
    X, A = x.astype(np.float64), a.astype(np.float64)
    y = np.zeros((N, 128, S * B)); h = np.zeros((128, B))
    for r in range(N):
        for s in range(S):
            h = np.tanh(A[r].T @ h + X[r][:, B * s:B * s + B])
            y[r][:, B * s:B * s + B] = h
    return {"y": y.astype(ml_dtypes.bfloat16)}

@@ -1,0 +1,265 @@
+from concourse.bass import DstId, RemoteDMATransfer
+from concourse.mybir import AluOpType, ActivationFunctionType
+
+S, B = 4, 256
+NB = 4
+BW = B // NB
+HW = B // 2
+NBANK = 8
+BF, F32 = "bfloat16", "float32"
+
+SCRATCH = {
+    "xn": ("sbuf", [128, S, NB, BW], BF),
+    "xb": ("sbuf", [128, NB, S, BW], BF),
+    "yb": ("sbuf", [128, NB, S, BW], BF),
+    "yn": ("sbuf", [128, S, NB, BW], BF),
+    "ab": ("sbuf", [128, 128], BF),
+    "ones": ("sbuf", [128, 128], BF),
+    "ident": ("sbuf", [128, 128], BF),
+    "xin": ("sbuf", [128, 6, S, BW], BF),
+    "zin": ("sbuf", [128, BW], BF),
+    "h3": ("sbuf", [128, BW], BF),
+    "hb": ("sbuf", [128, 24, BW], BF),
+    "x0": ("sbuf", [128, S * B], BF),
+    "y0": ("sbuf", [128, S * B], BF),
+    "zb": ("sbuf", [128, B], BF),
+}
+for _i in range(NBANK):
+    SCRATCH["ps%d" % _i] = ("psum", [128, 512], F32)
+
+SEMAPHORES = ["ld0", "ld1", "lda", "idm", "ids", "mm0", "mm1", "hs0", "hs1", "zs", "pm", "snd", "aarr", "zarr",
+              "xa1", "xa2", "xa3", "xa4", "xa5", "xa6", "yarr", "pa", "pb", "st", "rar", "rxr"]
+
+
+def _bits(m):
+    return [b for b in range(m.bit_length()) if (m >> b) & 1]
+
+
+def _n(m):
+    return len(_bits(m))
+
+
+def _split(topo, src, dests):
+    allowed = [_bits(topo.mask(src, d)) for d in dests]
+    few = min(len(a) for a in allowed)
+    tight = [i for i, a in enumerate(allowed) if len(a) == few]
+    loose = [i for i, a in enumerate(allowed) if len(a) > few]
+    groups = [(tight, allowed[tight[0]])]
+    if loose:
+        groups.append((loose, [b for b in allowed[loose[0]] if b not in allowed[tight[0]]]))
+    out = [0] * len(dests)
+    for idx, pool in groups:
+        k = 1
+        while 2 * k * len(idx) <= len(pool):
+            k *= 2
+        for n, i in enumerate(idx):
+            out[i] = sum(1 << b for b in pool[n * k:(n + 1) * k])
+    return out
+
+
+def _plan(T, topo):
+    R = list(T.cores)
+    allc = range(topo.CORES_PER_CHIP * topo.CHIPS)
+
+    def helpers(ch, targets):
+        return [c for c in allc if topo.chip(c) == ch and c not in R and all(topo.may_write(c, q) for q in targets)]
+
+    home = [r for r in range(len(R)) if r == 0 or topo.may_write(R[0], R[r])][:NB]
+    C = []
+    for j, r in enumerate(home):
+        cand = helpers(topo.chip(R[r]), R)
+        near = [c for c in cand if topo.die(c) == topo.die(R[r])]
+        far = [c for c in cand if topo.die(c) != topo.die(R[r])]
+        C.append((near if j % 2 == 0 else far)[0])
+    hop = {0: list(C)}
+    relay = {}
+    relayed = []
+    for r in range(1, len(R)):
+        if all(topo.may_write(R[r], c) for c in C):
+            hop[r] = list(C)
+            continue
+        relayed.append(r)
+        hs = helpers(topo.chip(R[r]), C)
+        near = [c for c in hs if topo.die(c) == topo.die(R[r])]
+        far = [c for c in hs if topo.die(c) != topo.die(R[r])]
+        jm = [j for j in range(NB) if topo.mates(topo.chip(R[r]), topo.chip(C[j]))]
+        j0 = jm[0] if jm else 0
+        mid = sorted([j for j in range(NB) if j != j0 and home[j] != 0], key=lambda j: (j - j0) % NB)
+        order = [j0] + mid + [j for j in range(NB) if j != j0 and home[j] == 0]
+        seats = near[:NB // 2] + far[:NB // 2]
+        hop[r] = [None] * NB
+        for k, j in enumerate(order):
+            hop[r][j] = seats[k]
+            relay[seats[k]] = (r, j)
+    masks = {r: _split(topo, R[r], hop[r]) for r in hop}
+    n = len(relayed)
+    cuts = [min(128, (128 * i // n + 7) // 8 * 8) for i in range(n + 1)]
+    cut = {r: (cuts[i], cuts[i + 1]) for i, r in enumerate(relayed)}
+    return R, C, hop, relay, relayed, masks, cut
+
+
+def _fused(g, topo, dests, masks, srcs, dsts, rsem, lsem):
+    tr = []
+    for d, m, s, o in zip(dests, masks, srcs, dsts):
+        rid, pid, _se = topo.addr(d)
+        tr.append(RemoteDMATransfer(dst_ids=[DstId(rid=rid, pnc=pid)], dma_engine_mask=m, remote_sem=rsem, src=s, dst=o))
+    g.remote_dma_fused(tr, local_sem=lsem)
+    return sum(_n(m) for m in masks)
+
+
+def _send(g, topo, src_core, dst_core, out_ap, in_ap, rsem, lsem):
+    rid, pid, _se = topo.addr(dst_core)
+    m = topo.mask(src_core, dst_core)
+    g.remote_dma(out_ap, in_ap, rsem, lsem, pid, rid, m)
+    return _n(m)
+
+
+def _identity(g, T):
+    g.vector.memset(T.ones[:], 1.0).then_inc(T.sem.idm, 1)
+    g.wait_ge(T.sem.idm, 1)
+    g.affine_select(T.ident[:], T.ones[:], [[-1, 128]], AluOpType.is_equal, 0.0, 0, 1).then_inc(T.sem.ids, 1)
+
+
+def _rank0(g, core, T, topo, P):
+    R, C, hop, relay, relayed, masks, cut = P
+    sem, pe, act, dve = T.sem, g.tensor, g.scalar, g.vector
+    tanh = ActivationFunctionType.Tanh
+    hs, mm = [sem.hs0, sem.hs1], [sem.mm0, sem.mm1]
+    g.sync.dma_start(T.x0[:, 0:B], T.x[:, 0:B]).then_inc(sem.ld0, 16)
+    act.dma_start(T.ab[:], T.a[:]).then_inc(sem.lda, 16)
+    g.sync.dma_start(T.x0[:, B:S * B], T.x[:, B:S * B]).then_inc(sem.ld1, 16)
+    _identity(g, T)
+
+    def cols(t, h):
+        return slice(B * t + HW * h, B * t + HW * h + HW)
+
+    def bank(t, h):
+        return T["ps%d" % ((t - 1) * 2 + h)][:, 0:HW]
+
+    act.wait_ge(sem.ld0, 16)
+    for h in range(2):
+        act.activation(T.y0[:, cols(0, h)], T.x0[:, cols(0, h)], tanh).then_inc(hs[h], 1)
+    pe.wait_ge(sem.ids, 1)
+    pe.wait_ge(sem.ld1, 16)
+    for t in range(1, S):
+        for h in range(2):
+            pe.matmul(bank(t, h), T.ident[:], T.x0[:, cols(t, h)], True, False)
+    pe.wait_ge(sem.lda, 16)
+    for t in range(1, S):
+        for h in range(2):
+            pe.wait_ge(hs[h], t)
+            pe.matmul(bank(t, h), T.ab[:], T.y0[:, cols(t - 1, h)], False, True).then_inc(mm[h], 1)
+    for t in range(1, S - 1):
+        for h in range(2):
+            act.wait_ge(mm[h], t)
+            act.activation(T.y0[:, cols(t, h)], bank(t, h), tanh).then_inc(hs[h], 1)
+    for h in range(2):
+        dve.wait_ge(mm[h], S - 1)
+        dve.tensor_copy(T.zb[:, HW * h:HW * h + HW], bank(S - 1, h)).then_inc(sem.zs, 1)
+    g.wait_ge(sem.zs, 2)
+    n = _fused(g, topo, hop[0], masks[0], [T.zb[:, BW * j:BW * j + BW] for j in range(NB)],
+               [T.zin[:] for j in range(NB)], sem.zarr, sem.snd)
+    act.wait_ge(sem.zs, 2)
+    for h in range(2):
+        act.activation(T.y0[:, cols(S - 1, h)], bank(S - 1, h), tanh).then_inc(hs[h], 1)
+    g.sync.wait_ge(hs[0], S)
+    g.sync.wait_ge(hs[1], S)
+    g.sync.dma_start(T.y[:], T.y0[:]).then_inc(sem.st, 16)
+    g.sync.wait_ge(sem.st, 16)
+    g.wait_ge(sem.snd, n)
+
+
+def _rank(g, core, T, topo, P, r):
+    R, C, hop, relay, relayed, masks, cut = P
+    sem, dve = T.sem, g.vector
+    sent = 0
+    g.sync.dma_start(T.xn[:], T.x[:]).then_inc(sem.ld0, 16)
+    if r in relayed:
+        c0, c1 = cut[r]
+        g.scalar.dma_start(T.ab[:, c0:c1], T.a[:, c0:c1]).then_inc(sem.lda, 16)
+        g.wait_ge(sem.lda, 16)
+        sent += _fused(g, topo, hop[r], masks[r], [T.ab[:, c0:c1]] * NB, [T.ab[:, c0:c1]] * NB, sem.rar, sem.snd)
+    dve.wait_ge(sem.ld0, 16)
+    for j in range(NB):
+        dve.tensor_copy(T.xb[:, j], T.xn[:, :, j, :]).then_inc(sem.pm, 1)
+    g.wait_ge(sem.pm, NB)
+    if r in relayed:
+        dsts, rsem = [T.xb[:, j] for j in range(NB)], sem.rxr
+    else:
+        dsts, rsem = [T.xin[:, r - 1] for j in range(NB)], sem["xa%d" % r]
+    sent += _fused(g, topo, hop[r], masks[r], [T.xb[:, j] for j in range(NB)], dsts, rsem, sem.snd)
+    dve.wait_ge(sem.yarr, sum(_n(topo.mask(c, core)) for c in C))
+    for s in range(S):
+        dve.tensor_copy(T.yn[:, s], T.yb[:, :, s, :]).then_inc(sem.pa if s < S // 2 else sem.pb, 1)
+    half = S * B // 2
+    g.sync.wait_ge(sem.pa, S // 2)
+    g.sync.dma_start(T.y[:, 0:half], T.yn[:, 0:S // 2]).then_inc(sem.st, 16)
+    g.scalar.wait_ge(sem.pb, S // 2)
+    g.scalar.dma_start(T.y[:, half:2 * half], T.yn[:, S // 2:S]).then_inc(sem.st, 16)
+    g.wait_ge(sem.snd, sent)
+    g.wait_ge(sem.st, 32)
+
+
+def _relay(g, core, T, topo, P):
+    R, C, hop, relay, relayed, masks, cut = P
+    sem = T.sem
+    r, j = relay[core]
+    c0, c1 = cut[r]
+    got = _n(masks[r][j])
+    g.wait_ge(sem.rar, got)
+    n = _send(g, topo, core, C[j], T.ab[:, c0:c1], T.ab[:, c0:c1], sem.aarr, sem.snd)
+    g.wait_ge(sem.rxr, got)
+    n += _send(g, topo, core, C[j], T.xin[:, r - 1], T.xb[:, j], sem["xa%d" % r], sem.snd)
+    g.wait_ge(sem.snd, n)
+
+
+def _compute(g, core, T, topo, P, j):
+    R, C, hop, relay, relayed, masks, cut = P
+    sem, pe, act = T.sem, g.tensor, g.scalar
+    tanh = ActivationFunctionType.Tanh
+    steps = S * (len(R) - 1)
+    _identity(g, T)
+
+    def bank(k):
+        return T["ps%d" % (k % NBANK)][:, 0:BW]
+
+    def arrives(r):
+        return _n(topo.mask(hop[r][j], core)) if r in relayed else _n(masks[r][j])
+
+    def put_x(k):
+        r, s = 1 + k // S, k % S
+        if s == 0:
+            pe.wait_ge(sem["xa%d" % r], arrives(r))
+        pe.matmul(bank(k), T.ident[:], T.xin[:, r - 1, s, :], True, False)
+
+    act.wait_ge(sem.zarr, _n(masks[0][j]))
+    act.activation(T.h3[:], T.zin[:], tanh).then_inc(sem.hs0, 1)
+    pe.wait_ge(sem.ids, 1)
+    put_x(0)
+    pe.wait_ge(sem.aarr, sum(_n(topo.mask(hop[r][j], core)) for r in relayed))
+    for k in range(steps):
+        pe.wait_ge(sem.hs0, k + 1)
+        pe.matmul(bank(k), T.ab[:], T.h3[:] if k == 0 else T.hb[:, k - 1, :], False, True).then_inc(sem.mm0, 1)
+        if k + 1 < steps:
+            put_x(k + 1)
+        act.wait_ge(sem.mm0, k + 1)
+        act.activation(T.hb[:, k, :], bank(k), tanh).then_inc(sem.hs0, 1)
+    n = 0
+    for r in range(1, len(R)):
+        g.wait_ge(sem.hs0, 1 + S * r)
+        n += _send(g, topo, core, R[r], T.yb[:, j], T.hb[:, S * (r - 1):S * r, :], sem.yarr, sem.snd)
+    g.wait_ge(sem.snd, n)
+
+
+def rank_program(g, core, T, topo):
+    P = _plan(T, topo)
+    R, C, relay = P[0], P[1], P[3]
+    rank = T.rank_of(core)
+    if rank == 0:
+        _rank0(g, core, T, topo, P)
+    elif rank is not None:
+        _rank(g, core, T, topo, P, rank)
+    elif core in C:
+        _compute(g, core, T, topo, P, C.index(core))
+    elif core in relay:
+        _relay(g, core, T, topo, P)

@@ -5,7 +5,9 @@ S, B = 4, 256
 NB = 4
 BW = B // NB
 HW = B // 2
+H2 = S // 2
 NBANK = 8
+Q = 100
 BF, F32 = "bfloat16", "float32"
 
 SCRATCH = {
@@ -16,6 +18,7 @@ SCRATCH = {
     "ab": ("sbuf", [128, 128], BF),
     "ones": ("sbuf", [128, 128], BF),
     "ident": ("sbuf", [128, 128], BF),
+    "idr": ("sbuf", [128, 128], BF),
     "xin": ("sbuf", [128, 6, S, BW], BF),
     "zin": ("sbuf", [128, BW], BF),
     "h3": ("sbuf", [128, BW], BF),
@@ -28,7 +31,8 @@ for _i in range(NBANK):
     SCRATCH["ps%d" % _i] = ("psum", [128, 512], F32)
 
 SEMAPHORES = ["ld0", "ld1", "lda", "idm", "ids", "mm0", "mm1", "hs0", "hs1", "zs", "pm", "snd", "aarr", "zarr",
-              "xa1", "xa2", "xa3", "xa4", "xa5", "xa6", "yarr", "pa", "pb", "st", "rar", "rxr"]
+              "xa1", "xa2", "xa3", "xa4", "xa5", "xa6", "yarr", "yar2", "pa", "pb", "pc", "st", "rar", "rxr", "rir",
+              "iarr"]
 
 
 def _bits(m):
@@ -55,6 +59,16 @@ def _split(topo, src, dests):
         for n, i in enumerate(idx):
             out[i] = sum(1 << b for b in pool[n * k:(n + 1) * k])
     return out
+
+
+def _cuts(owners):
+    n = len(owners)
+    c = [128 * i // n for i in range(n + 1)]
+    return {r: (c[i], c[i + 1]) for i, r in enumerate(owners)}
+
+
+def _segs(r, nranks):
+    return [(0, H2), (H2, S)] if r == nranks - 1 else [(0, S)]
 
 
 def _plan(T, topo):
@@ -92,10 +106,9 @@ def _plan(T, topo):
             hop[r][j] = seats[k]
             relay[seats[k]] = (r, j)
     masks = {r: _split(topo, R[r], hop[r]) for r in hop}
-    n = len(relayed)
-    cuts = [min(128, (128 * i // n + 7) // 8 * 8) for i in range(n + 1)]
-    cut = {r: (cuts[i], cuts[i + 1]) for i, r in enumerate(relayed)}
-    return R, C, hop, relay, relayed, masks, cut
+    cut = _cuts(relayed[1:])
+    icut = _cuts(list(range(len(R))) + [Q + r for r in relayed])
+    return R, C, hop, relay, relayed, masks, cut, icut
 
 
 def _fused(g, topo, dests, masks, srcs, dsts, rsem, lsem):
@@ -114,21 +127,25 @@ def _send(g, topo, src_core, dst_core, out_ap, in_ap, rsem, lsem):
     return _n(m)
 
 
-def _identity(g, T):
-    g.vector.memset(T.ones[:], 1.0).then_inc(T.sem.idm, 1)
+def _identity(g, T, c0, c1):
+    g.vector.memset(T.ones[:, c0:c1], 1.0).then_inc(T.sem.idm, 1)
     g.wait_ge(T.sem.idm, 1)
-    g.affine_select(T.ident[:], T.ones[:], [[-1, 128]], AluOpType.is_equal, 0.0, 0, 1).then_inc(T.sem.ids, 1)
+    g.affine_select(T.ident[:, c0:c1], T.ones[:, c0:c1], [[-1, c1 - c0]], AluOpType.is_equal, 0.0, -c0,
+                    1).then_inc(T.sem.ids, 1)
+    g.wait_ge(T.sem.ids, 1)
 
 
 def _rank0(g, core, T, topo, P):
-    R, C, hop, relay, relayed, masks, cut = P
+    R, C, hop, relay, relayed, masks, cut, icut = P
     sem, pe, act, dve = T.sem, g.tensor, g.scalar, g.vector
     tanh = ActivationFunctionType.Tanh
     hs, mm = [sem.hs0, sem.hs1], [sem.mm0, sem.mm1]
     g.sync.dma_start(T.x0[:, 0:B], T.x[:, 0:B]).then_inc(sem.ld0, 16)
     act.dma_start(T.ab[:], T.a[:]).then_inc(sem.lda, 16)
     g.sync.dma_start(T.x0[:, B:S * B], T.x[:, B:S * B]).then_inc(sem.ld1, 16)
-    _identity(g, T)
+    _identity(g, T, 0, 128)
+    i0, i1 = icut[0]
+    n = _fused(g, topo, hop[0], masks[0], [T.ident[:, i0:i1]] * NB, [T.ident[:, i0:i1]] * NB, sem.iarr, sem.snd)
 
     def cols(t, h):
         return slice(B * t + HW * h, B * t + HW * h + HW)
@@ -157,8 +174,8 @@ def _rank0(g, core, T, topo, P):
         dve.wait_ge(mm[h], S - 1)
         dve.tensor_copy(T.zb[:, HW * h:HW * h + HW], bank(S - 1, h)).then_inc(sem.zs, 1)
     g.wait_ge(sem.zs, 2)
-    n = _fused(g, topo, hop[0], masks[0], [T.zb[:, BW * j:BW * j + BW] for j in range(NB)],
-               [T.zin[:] for j in range(NB)], sem.zarr, sem.snd)
+    n += _fused(g, topo, hop[0], masks[0], [T.zb[:, BW * j:BW * j + BW] for j in range(NB)],
+                [T.zin[:] for j in range(NB)], sem.zarr, sem.snd)
     act.wait_ge(sem.zs, 2)
     for h in range(2):
         act.activation(T.y0[:, cols(S - 1, h)], bank(S - 1, h), tanh).then_inc(hs[h], 1)
@@ -170,55 +187,72 @@ def _rank0(g, core, T, topo, P):
 
 
 def _rank(g, core, T, topo, P, r):
-    R, C, hop, relay, relayed, masks, cut = P
+    R, C, hop, relay, relayed, masks, cut, icut = P
     sem, dve = T.sem, g.vector
     sent = 0
     g.sync.dma_start(T.xn[:], T.x[:]).then_inc(sem.ld0, 16)
-    if r in relayed:
+    if r in cut:
         c0, c1 = cut[r]
         g.scalar.dma_start(T.ab[:, c0:c1], T.a[:, c0:c1]).then_inc(sem.lda, 16)
+    i0, i1 = icut[r]
+    _identity(g, T, i0, i1)
+    if r in relayed:
+        sent += _fused(g, topo, hop[r], masks[r], [T.ident[:, i0:i1]] * NB, [T.idr[:, i0:i1]] * NB, sem.rir, sem.snd)
+    else:
+        sent += _fused(g, topo, hop[r], masks[r], [T.ident[:, i0:i1]] * NB, [T.ident[:, i0:i1]] * NB, sem.iarr, sem.snd)
+    if r in cut:
         g.wait_ge(sem.lda, 16)
         sent += _fused(g, topo, hop[r], masks[r], [T.ab[:, c0:c1]] * NB, [T.ab[:, c0:c1]] * NB, sem.rar, sem.snd)
     dve.wait_ge(sem.ld0, 16)
-    for j in range(NB):
-        dve.tensor_copy(T.xb[:, j], T.xn[:, :, j, :]).then_inc(sem.pm, 1)
-    g.wait_ge(sem.pm, NB)
+    for s in range(S):
+        dve.tensor_copy(T.xb[:, :, s, :], T.xn[:, s]).then_inc(sem.pm, 1)
+    g.wait_ge(sem.pm, S)
     if r in relayed:
         dsts, rsem = [T.xb[:, j] for j in range(NB)], sem.rxr
     else:
         dsts, rsem = [T.xin[:, r - 1] for j in range(NB)], sem["xa%d" % r]
     sent += _fused(g, topo, hop[r], masks[r], [T.xb[:, j] for j in range(NB)], dsts, rsem, sem.snd)
-    dve.wait_ge(sem.yarr, sum(_n(topo.mask(c, core)) for c in C))
-    for s in range(S):
-        dve.tensor_copy(T.yn[:, s], T.yb[:, :, s, :]).then_inc(sem.pa if s < S // 2 else sem.pb, 1)
-    half = S * B // 2
-    g.sync.wait_ge(sem.pa, S // 2)
-    g.sync.dma_start(T.y[:, 0:half], T.yn[:, 0:S // 2]).then_inc(sem.st, 16)
-    g.scalar.wait_ge(sem.pb, S // 2)
-    g.scalar.dma_start(T.y[:, half:2 * half], T.yn[:, S // 2:S]).then_inc(sem.st, 16)
+    per = sum(_n(topo.mask(c, core)) for c in C)
+    turned = [sem.pa, sem.pa, sem.pb, sem.pc]
+    for i, (s0, s1) in enumerate(_segs(r, len(R))):
+        dve.wait_ge([sem.yarr, sem.yar2][i], per)
+        for s in range(s0, s1):
+            dve.tensor_copy(T.yn[:, s], T.yb[:, :, s, :]).then_inc(turned[s], 1)
+    g.sync.wait_ge(sem.pa, 2)
+    g.sync.dma_start(T.y[:, 0:2 * B], T.yn[:, 0:2]).then_inc(sem.st, 16)
+    g.sync.wait_ge(sem.pb, 1)
+    g.sync.dma_start(T.y[:, 2 * B:3 * B], T.yn[:, 2]).then_inc(sem.st, 16)
+    g.scalar.wait_ge(sem.pc, 1)
+    g.scalar.dma_start(T.y[:, 3 * B:4 * B], T.yn[:, 3]).then_inc(sem.st, 16)
     g.wait_ge(sem.snd, sent)
-    g.wait_ge(sem.st, 32)
+    g.wait_ge(sem.st, 48)
 
 
 def _relay(g, core, T, topo, P):
-    R, C, hop, relay, relayed, masks, cut = P
+    R, C, hop, relay, relayed, masks, cut, icut = P
     sem = T.sem
     r, j = relay[core]
-    c0, c1 = cut[r]
     got = _n(masks[r][j])
-    g.wait_ge(sem.rar, got)
-    n = _send(g, topo, core, C[j], T.ab[:, c0:c1], T.ab[:, c0:c1], sem.aarr, sem.snd)
+    q0, q1 = icut[Q + r]
+    _identity(g, T, q0, q1)
+    n = _send(g, topo, core, C[j], T.ident[:, q0:q1], T.ident[:, q0:q1], sem.iarr, sem.snd)
+    i0, i1 = icut[r]
+    g.wait_ge(sem.rir, got)
+    n += _send(g, topo, core, C[j], T.ident[:, i0:i1], T.idr[:, i0:i1], sem.iarr, sem.snd)
+    if r in cut:
+        c0, c1 = cut[r]
+        g.wait_ge(sem.rar, got)
+        n += _send(g, topo, core, C[j], T.ab[:, c0:c1], T.ab[:, c0:c1], sem.aarr, sem.snd)
     g.wait_ge(sem.rxr, got)
     n += _send(g, topo, core, C[j], T.xin[:, r - 1], T.xb[:, j], sem["xa%d" % r], sem.snd)
     g.wait_ge(sem.snd, n)
 
 
 def _compute(g, core, T, topo, P, j):
-    R, C, hop, relay, relayed, masks, cut = P
+    R, C, hop, relay, relayed, masks, cut, icut = P
     sem, pe, act = T.sem, g.tensor, g.scalar
     tanh = ActivationFunctionType.Tanh
     steps = S * (len(R) - 1)
-    _identity(g, T)
 
     def bank(k):
         return T["ps%d" % (k % NBANK)][:, 0:BW]
@@ -232,11 +266,11 @@ def _compute(g, core, T, topo, P, j):
             pe.wait_ge(sem["xa%d" % r], arrives(r))
         pe.matmul(bank(k), T.ident[:], T.xin[:, r - 1, s, :], True, False)
 
-    act.wait_ge(sem.zarr, _n(masks[0][j]))
+    act.wait_ge(sem.zarr, arrives(0))
     act.activation(T.h3[:], T.zin[:], tanh).then_inc(sem.hs0, 1)
-    pe.wait_ge(sem.ids, 1)
+    pe.wait_ge(sem.iarr, sum(arrives(r % Q) for r in icut))
     put_x(0)
-    pe.wait_ge(sem.aarr, sum(_n(topo.mask(hop[r][j], core)) for r in relayed))
+    pe.wait_ge(sem.aarr, sum(arrives(r) for r in cut))
     for k in range(steps):
         pe.wait_ge(sem.hs0, k + 1)
         pe.matmul(bank(k), T.ab[:], T.h3[:] if k == 0 else T.hb[:, k - 1, :], False, True).then_inc(sem.mm0, 1)
@@ -246,8 +280,11 @@ def _compute(g, core, T, topo, P, j):
         act.activation(T.hb[:, k, :], bank(k), tanh).then_inc(sem.hs0, 1)
     n = 0
     for r in range(1, len(R)):
-        g.wait_ge(sem.hs0, 1 + S * r)
-        n += _send(g, topo, core, R[r], T.yb[:, j], T.hb[:, S * (r - 1):S * r, :], sem.yarr, sem.snd)
+        k0 = S * (r - 1)
+        for i, (s0, s1) in enumerate(_segs(r, len(R))):
+            g.wait_ge(sem.hs0, 1 + k0 + s1)
+            n += _send(g, topo, core, R[r], T.yb[:, j, s0:s1, :], T.hb[:, k0 + s0:k0 + s1, :],
+                       [sem.yarr, sem.yar2][i], sem.snd)
     g.wait_ge(sem.snd, n)
 
 

from concourse.bass import DstId, RemoteDMATransfer
from concourse.mybir import AluOpType, ActivationFunctionType

S, B = 4, 256
NB = 4
BW = B // NB
HW = B // 2
H2 = S // 2
NBANK = 8
Q = 100
BF, F32 = "bfloat16", "float32"

SCRATCH = {
    "xn": ("sbuf", [128, S, NB, BW], BF),
    "xb": ("sbuf", [128, NB, S, BW], BF),
    "yb": ("sbuf", [128, NB, S, BW], BF),
    "yn": ("sbuf", [128, S, NB, BW], BF),
    "ab": ("sbuf", [128, 128], BF),
    "ones": ("sbuf", [128, 128], BF),
    "ident": ("sbuf", [128, 128], BF),
    "idr": ("sbuf", [128, 128], BF),
    "xin": ("sbuf", [128, 6, S, BW], BF),
    "zin": ("sbuf", [128, BW], BF),
    "h3": ("sbuf", [128, BW], BF),
    "hb": ("sbuf", [128, 24, BW], BF),
    "x0": ("sbuf", [128, S * B], BF),
    "y0": ("sbuf", [128, S * B], BF),
    "zb": ("sbuf", [128, B], BF),
}
for _i in range(NBANK):
    SCRATCH["ps%d" % _i] = ("psum", [128, 512], F32)

SEMAPHORES = ["ld0", "ld1", "lda", "idm", "ids", "mm0", "mm1", "hs0", "hs1", "zs", "pm", "snd", "aarr", "zarr",
              "xa1", "xa2", "xa3", "xa4", "xa5", "xa6", "yarr", "yar2", "pa", "pb", "pc", "st", "rar", "rxr", "rir",
              "iarr"]


def _bits(m):
    return [b for b in range(m.bit_length()) if (m >> b) & 1]


def _n(m):
    return len(_bits(m))


def _split(topo, src, dests):
    allowed = [_bits(topo.mask(src, d)) for d in dests]
    few = min(len(a) for a in allowed)
    tight = [i for i, a in enumerate(allowed) if len(a) == few]
    loose = [i for i, a in enumerate(allowed) if len(a) > few]
    groups = [(tight, allowed[tight[0]])]
    if loose:
        groups.append((loose, [b for b in allowed[loose[0]] if b not in allowed[tight[0]]]))
    out = [0] * len(dests)
    for idx, pool in groups:
        k = 1
        while 2 * k * len(idx) <= len(pool):
            k *= 2
        for n, i in enumerate(idx):
            out[i] = sum(1 << b for b in pool[n * k:(n + 1) * k])
    return out


def _cuts(owners):
    n = len(owners)
    c = [128 * i // n for i in range(n + 1)]
    return {r: (c[i], c[i + 1]) for i, r in enumerate(owners)}


def _segs(r, nranks):
    return [(0, H2), (H2, S)] if r == nranks - 1 else [(0, S)]


def _plan(T, topo):
    R = list(T.cores)
    allc = range(topo.CORES_PER_CHIP * topo.CHIPS)

    def helpers(ch, targets):
        return [c for c in allc if topo.chip(c) == ch and c not in R and all(topo.may_write(c, q) for q in targets)]

    home = [r for r in range(len(R)) if r == 0 or topo.may_write(R[0], R[r])][:NB]
    C = []
    for j, r in enumerate(home):
        cand = helpers(topo.chip(R[r]), R)
        near = [c for c in cand if topo.die(c) == topo.die(R[r])]
        far = [c for c in cand if topo.die(c) != topo.die(R[r])]
        C.append((near if j % 2 == 0 else far)[0])
    hop = {0: list(C)}
    relay = {}
    relayed = []
    for r in range(1, len(R)):
        if all(topo.may_write(R[r], c) for c in C):
            hop[r] = list(C)
            continue
        relayed.append(r)
        hs = helpers(topo.chip(R[r]), C)
        near = [c for c in hs if topo.die(c) == topo.die(R[r])]
        far = [c for c in hs if topo.die(c) != topo.die(R[r])]
        jm = [j for j in range(NB) if topo.mates(topo.chip(R[r]), topo.chip(C[j]))]
        j0 = jm[0] if jm else 0
        mid = sorted([j for j in range(NB) if j != j0 and home[j] != 0], key=lambda j: (j - j0) % NB)
        order = [j0] + mid + [j for j in range(NB) if j != j0 and home[j] == 0]
        seats = near[:NB // 2] + far[:NB // 2]
        hop[r] = [None] * NB
        for k, j in enumerate(order):
            hop[r][j] = seats[k]
            relay[seats[k]] = (r, j)
    masks = {r: _split(topo, R[r], hop[r]) for r in hop}
    cut = _cuts(relayed[1:])
    icut = _cuts(list(range(len(R))) + [Q + r for r in relayed])
    return R, C, hop, relay, relayed, masks, cut, icut


def _fused(g, topo, dests, masks, srcs, dsts, rsem, lsem):
    tr = []
    for d, m, s, o in zip(dests, masks, srcs, dsts):
        rid, pid, _se = topo.addr(d)
        tr.append(RemoteDMATransfer(dst_ids=[DstId(rid=rid, pnc=pid)], dma_engine_mask=m, remote_sem=rsem, src=s, dst=o))
    g.remote_dma_fused(tr, local_sem=lsem)
    return sum(_n(m) for m in masks)


def _send(g, topo, src_core, dst_core, out_ap, in_ap, rsem, lsem):
    rid, pid, _se = topo.addr(dst_core)
    m = topo.mask(src_core, dst_core)
    g.remote_dma(out_ap, in_ap, rsem, lsem, pid, rid, m)
    return _n(m)


def _identity(g, T, c0, c1):
    g.vector.memset(T.ones[:, c0:c1], 1.0).then_inc(T.sem.idm, 1)
    g.wait_ge(T.sem.idm, 1)
    g.affine_select(T.ident[:, c0:c1], T.ones[:, c0:c1], [[-1, c1 - c0]], AluOpType.is_equal, 0.0, -c0,
                    1).then_inc(T.sem.ids, 1)
    g.wait_ge(T.sem.ids, 1)


def _rank0(g, core, T, topo, P):
    R, C, hop, relay, relayed, masks, cut, icut = P
    sem, pe, act, dve = T.sem, g.tensor, g.scalar, g.vector
    tanh = ActivationFunctionType.Tanh
    hs, mm = [sem.hs0, sem.hs1], [sem.mm0, sem.mm1]
    g.sync.dma_start(T.x0[:, 0:B], T.x[:, 0:B]).then_inc(sem.ld0, 16)
    act.dma_start(T.ab[:], T.a[:]).then_inc(sem.lda, 16)
    g.sync.dma_start(T.x0[:, B:S * B], T.x[:, B:S * B]).then_inc(sem.ld1, 16)
    _identity(g, T, 0, 128)
    i0, i1 = icut[0]
    n = _fused(g, topo, hop[0], masks[0], [T.ident[:, i0:i1]] * NB, [T.ident[:, i0:i1]] * NB, sem.iarr, sem.snd)

    def cols(t, h):
        return slice(B * t + HW * h, B * t + HW * h + HW)

    def bank(t, h):
        return T["ps%d" % ((t - 1) * 2 + h)][:, 0:HW]

    act.wait_ge(sem.ld0, 16)
    for h in range(2):
        act.activation(T.y0[:, cols(0, h)], T.x0[:, cols(0, h)], tanh).then_inc(hs[h], 1)
    pe.wait_ge(sem.ids, 1)
    pe.wait_ge(sem.ld1, 16)
    for t in range(1, S):
        for h in range(2):
            pe.matmul(bank(t, h), T.ident[:], T.x0[:, cols(t, h)], True, False)
    pe.wait_ge(sem.lda, 16)
    for t in range(1, S):
        for h in range(2):
            pe.wait_ge(hs[h], t)
            pe.matmul(bank(t, h), T.ab[:], T.y0[:, cols(t - 1, h)], False, True).then_inc(mm[h], 1)
    for t in range(1, S - 1):
        for h in range(2):
            act.wait_ge(mm[h], t)
            act.activation(T.y0[:, cols(t, h)], bank(t, h), tanh).then_inc(hs[h], 1)
    for h in range(2):
        dve.wait_ge(mm[h], S - 1)
        dve.tensor_copy(T.zb[:, HW * h:HW * h + HW], bank(S - 1, h)).then_inc(sem.zs, 1)
    g.wait_ge(sem.zs, 2)
    n += _fused(g, topo, hop[0], masks[0], [T.zb[:, BW * j:BW * j + BW] for j in range(NB)],
                [T.zin[:] for j in range(NB)], sem.zarr, sem.snd)
    act.wait_ge(sem.zs, 2)
    for h in range(2):
        act.activation(T.y0[:, cols(S - 1, h)], bank(S - 1, h), tanh).then_inc(hs[h], 1)
    g.sync.wait_ge(hs[0], S)
    g.sync.wait_ge(hs[1], S)
    g.sync.dma_start(T.y[:], T.y0[:]).then_inc(sem.st, 16)
    g.sync.wait_ge(sem.st, 16)
    g.wait_ge(sem.snd, n)


def _rank(g, core, T, topo, P, r):
    R, C, hop, relay, relayed, masks, cut, icut = P
    sem, dve = T.sem, g.vector
    sent = 0
    g.sync.dma_start(T.xn[:], T.x[:]).then_inc(sem.ld0, 16)
    if r in cut:
        c0, c1 = cut[r]
        g.scalar.dma_start(T.ab[:, c0:c1], T.a[:, c0:c1]).then_inc(sem.lda, 16)
    i0, i1 = icut[r]
    _identity(g, T, i0, i1)
    if r in relayed:
        sent += _fused(g, topo, hop[r], masks[r], [T.ident[:, i0:i1]] * NB, [T.idr[:, i0:i1]] * NB, sem.rir, sem.snd)
    else:
        sent += _fused(g, topo, hop[r], masks[r], [T.ident[:, i0:i1]] * NB, [T.ident[:, i0:i1]] * NB, sem.iarr, sem.snd)
    if r in cut:
        g.wait_ge(sem.lda, 16)
        sent += _fused(g, topo, hop[r], masks[r], [T.ab[:, c0:c1]] * NB, [T.ab[:, c0:c1]] * NB, sem.rar, sem.snd)
    dve.wait_ge(sem.ld0, 16)
    for s in range(S):
        dve.tensor_copy(T.xb[:, :, s, :], T.xn[:, s]).then_inc(sem.pm, 1)
    g.wait_ge(sem.pm, S)
    if r in relayed:
        dsts, rsem = [T.xb[:, j] for j in range(NB)], sem.rxr
    else:
        dsts, rsem = [T.xin[:, r - 1] for j in range(NB)], sem["xa%d" % r]
    sent += _fused(g, topo, hop[r], masks[r], [T.xb[:, j] for j in range(NB)], dsts, rsem, sem.snd)
    per = sum(_n(topo.mask(c, core)) for c in C)
    turned = [sem.pa, sem.pa, sem.pb, sem.pc]
    for i, (s0, s1) in enumerate(_segs(r, len(R))):
        dve.wait_ge([sem.yarr, sem.yar2][i], per)
        for s in range(s0, s1):
            dve.tensor_copy(T.yn[:, s], T.yb[:, :, s, :]).then_inc(turned[s], 1)
    g.sync.wait_ge(sem.pa, 2)
    g.sync.dma_start(T.y[:, 0:2 * B], T.yn[:, 0:2]).then_inc(sem.st, 16)
    g.sync.wait_ge(sem.pb, 1)
    g.sync.dma_start(T.y[:, 2 * B:3 * B], T.yn[:, 2]).then_inc(sem.st, 16)
    g.scalar.wait_ge(sem.pc, 1)
    g.scalar.dma_start(T.y[:, 3 * B:4 * B], T.yn[:, 3]).then_inc(sem.st, 16)
    g.wait_ge(sem.snd, sent)
    g.wait_ge(sem.st, 48)


def _relay(g, core, T, topo, P):
    R, C, hop, relay, relayed, masks, cut, icut = P
    sem = T.sem
    r, j = relay[core]
    got = _n(masks[r][j])
    q0, q1 = icut[Q + r]
    _identity(g, T, q0, q1)
    n = _send(g, topo, core, C[j], T.ident[:, q0:q1], T.ident[:, q0:q1], sem.iarr, sem.snd)
    i0, i1 = icut[r]
    g.wait_ge(sem.rir, got)
    n += _send(g, topo, core, C[j], T.ident[:, i0:i1], T.idr[:, i0:i1], sem.iarr, sem.snd)
    if r in cut:
        c0, c1 = cut[r]
        g.wait_ge(sem.rar, got)
        n += _send(g, topo, core, C[j], T.ab[:, c0:c1], T.ab[:, c0:c1], sem.aarr, sem.snd)
    g.wait_ge(sem.rxr, got)
    n += _send(g, topo, core, C[j], T.xin[:, r - 1], T.xb[:, j], sem["xa%d" % r], sem.snd)
    g.wait_ge(sem.snd, n)


def _compute(g, core, T, topo, P, j):
    R, C, hop, relay, relayed, masks, cut, icut = P
    sem, pe, act = T.sem, g.tensor, g.scalar
    tanh = ActivationFunctionType.Tanh
    steps = S * (len(R) - 1)

    def bank(k):
        return T["ps%d" % (k % NBANK)][:, 0:BW]

    def arrives(r):
        return _n(topo.mask(hop[r][j], core)) if r in relayed else _n(masks[r][j])

    def put_x(k):
        r, s = 1 + k // S, k % S
        if s == 0:
            pe.wait_ge(sem["xa%d" % r], arrives(r))
        pe.matmul(bank(k), T.ident[:], T.xin[:, r - 1, s, :], True, False)

    act.wait_ge(sem.zarr, arrives(0))
    act.activation(T.h3[:], T.zin[:], tanh).then_inc(sem.hs0, 1)
    pe.wait_ge(sem.iarr, sum(arrives(r % Q) for r in icut))
    put_x(0)
    pe.wait_ge(sem.aarr, sum(arrives(r) for r in cut))
    for k in range(steps):
        pe.wait_ge(sem.hs0, k + 1)
        pe.matmul(bank(k), T.ab[:], T.h3[:] if k == 0 else T.hb[:, k - 1, :], False, True).then_inc(sem.mm0, 1)
        if k + 1 < steps:
            put_x(k + 1)
        act.wait_ge(sem.mm0, k + 1)
        act.activation(T.hb[:, k, :], bank(k), tanh).then_inc(sem.hs0, 1)
    n = 0
    for r in range(1, len(R)):
        k0 = S * (r - 1)
        for i, (s0, s1) in enumerate(_segs(r, len(R))):
            g.wait_ge(sem.hs0, 1 + k0 + s1)
            n += _send(g, topo, core, R[r], T.yb[:, j, s0:s1, :], T.hb[:, k0 + s0:k0 + s1, :],
                       [sem.yarr, sem.yar2][i], sem.snd)
    g.wait_ge(sem.snd, n)


def rank_program(g, core, T, topo):
    P = _plan(T, topo)
    R, C, relay = P[0], P[1], P[3]
    rank = T.rank_of(core)
    if rank == 0:
        _rank0(g, core, T, topo, P)
    elif rank is not None:
        _rank(g, core, T, topo, P, rank)
    elif core in C:
        _compute(g, core, T, topo, P, C.index(core))
    elif core in relay:
        _relay(g, core, T, topo, P)
